import numpy as np
import ml_dtypes


def mxq(x, axis, fmt="e4m3"):
    dtype, down = {"e4m3": (ml_dtypes.float8_e4m3fn, 7), "e5m2": (ml_dtypes.float8_e5m2, 14)}[fmt]
    v = np.moveaxis(np.asarray(x, np.float32).astype(ml_dtypes.bfloat16).astype(np.float64), axis, -1)
    blocks = v.reshape(v.shape[:-1] + (-1, 32))
    amax = np.abs(blocks).max(-1, keepdims=True)
    byte = np.maximum(np.where(amax > 0, np.frexp(amax)[1] - 1 + 127, 0) - down, 1)
    scale = np.exp2(byte - 127.0)
    codes = (blocks / scale).astype(np.float32).astype(dtype).astype(np.float64)
    return np.moveaxis((codes * scale).reshape(v.shape), -1, axis)


WIDE = False


def mx_kscale(k):
    if not WIDE:
        return np.ones(k)
    levels = np.array([10, -10, 5, -5, 0])
    if k % 512:
        return np.exp2(np.random.permutation(np.resize(levels, k // 32))).repeat(32)
    a = np.empty((k // 512, 16))
    for p in range(k // 512):
        a[p, :8] = np.random.permutation(np.resize(levels, 8))
        for g in range(8):
            far = levels[np.abs(levels - a[p, g]) >= 10]
            a[p, g + 8] = far[np.random.randint(len(far))]
    return np.exp2(a.ravel()).repeat(32)


def f64(x):
    return np.asarray(x).astype(np.float64)


def striped(idx):
    return np.tile(idx.reshape(-1, 16).T, (8, 1)).astype(np.uint16)


def unstriped(offs):
    return offs[:16].T.reshape(-1).astype(np.int64)


K, T, D, V, H, N = 512, 512, 4, 256, 1024, 512
P = 2 ** 7


def setup_inputs():
    n = np.random.standard_normal
    s = mx_kscale(K)[:, None]
    u = mx_kscale(H)
    return {
        "xT": (n((K, T)) * s).astype(np.float32),
        "w1": (n((K, H)) / np.sqrt(K) / s * u).astype(np.float32),
        "w2": (n((H, N)) / np.sqrt(H) / u[:, None]).astype(np.float32),
        "gate": np.tile(np.random.uniform(0.2, 1.0, (D, 1, V)) / np.sqrt(D), (1, P, 1)).astype(np.float32),
        "pos1": striped(np.random.permutation(T)[:V]),
        "pos2": striped(np.random.permutation(T)[:V]),
        "pos3": striped(np.random.permutation(T)[:V]),
        "pos4": striped(np.random.permutation(T)[:V]),
    }


def reference(xT, w1, w2, gate, pos1, pos2, pos3, pos4):
    h = mxq(f64(w1), 0, "e4m3").T @ mxq(f64(xT), 0, "e4m3")
    z = sum(f64(gate)[d, :1] * h[:, unstriped(p)] for d, p in enumerate((pos1, pos2, pos3, pos4)))
    return mxq(f64(w2), 0, "e4m3").T @ mxq(z, 0, "e4m3")

@@ -1,0 +1,238 @@
+from contextlib import ExitStack
+
+import concourse.mybir as mybir
+
+F32 = mybir.dt.float32
+BF16 = mybir.dt.bfloat16
+U32 = mybir.dt.uint32
+U16 = mybir.dt.uint16
+U8 = mybir.dt.uint8
+FP8X4 = mybir.dt.float8_e4m3fn_x4
+MULT = mybir.AluOpType.mult
+ADD = mybir.AluOpType.add
+
+K, T, D, V, H, N = 512, 512, 4, 256, 1024, 512
+FLOPS = 2 * K * H * T + 2 * H * N * V
+
+P = 128
+J = 4
+KP = P * J
+X_CHUNKS = ((0, 256), (256, 384), (384, 512))
+WC = 256
+VH = 128
+
+
+def tile_picked_gcn_mlp_none_sub_l_kernel(tc, xT, w1, w2, gate, pos1, pos2, pos3, pos4, out):
+    nc = tc.nc
+    with ExitStack() as ctx:
+        lists = ctx.enter_context(tc.tile_pool(name="lists", bufs=1))
+        keep = ctx.enter_context(tc.tile_pool(name="keep", bufs=1))
+        psum = ctx.enter_context(tc.psum_pool(name="psum", bufs=8))
+
+        pos = [lists.tile([P, V // 16], U16, name=f"pos{d}") for d in range(D)]
+        gates = [keep.tile([P, V], F32, name=f"gate{d}") for d in range(D)]
+
+        x_raw = [keep.tile([P, J, b - a], F32, name=f"x_raw{a}") for a, b in X_CHUNKS]
+        w1_raw = [[keep.tile([P, J, WC], F32, name=f"w1_raw{g}_{c}") for c in range(2)] for g in range(2)]
+        w2_raw = [keep.tile([P, J, N], F32, name=f"w2_raw{g}") for g in range(2)]
+
+        x_view = xT.rearrange("(p j) t -> p j t", j=J)
+        w1_view = w1.rearrange("(p j) i -> p j i", j=J)
+        w2_view = w2.rearrange("(g p j) n -> g p j n", g=2, j=J)
+        out_view = out.rearrange("(a p) v -> p a v", p=P)
+
+        def load_w1(g, c):
+            i0 = g * KP + c * WC
+            nc.sync.dma_start(w1_raw[g][c][:], w1_view[:, :, i0 : i0 + WC])
+
+        def load_x(c):
+            a, b = X_CHUNKS[c]
+            nc.sync.dma_start(x_raw[c][:], x_view[:, :, a:b])
+
+        load_w1(0, 0)
+        load_w1(0, 1)
+        load_x(0)
+        nc.sync.dma_start(pos[0][:], pos1)
+        load_x(1)
+        load_x(2)
+        nc.sync.dma_start(gates[0][:], gate[0])
+        for d, src in ((1, pos2), (2, pos3), (3, pos4)):
+            nc.sync.dma_start(pos[d][:], src)
+            nc.sync.dma_start(gates[d][:], gate[d])
+        load_w1(1, 0)
+        load_w1(1, 1)
+        for g in range(2):
+            nc.sync.dma_start(w2_raw[g][:], w2_view[g])
+
+        w1_grouped = [keep.tile([P, J, P, J], BF16, name=f"w1_grouped{g}", align_bytes=64) for g in range(2)]
+        w1_codes = [keep.tile([P, J, P], U32, name=f"w1_codes{g}", align_bytes=64) for g in range(2)]
+        w1_scales = [keep.tile([P, J, P], U8, name=f"w1_scales{g}", align_bytes=64) for g in range(2)]
+        x_grouped = [keep.tile([P, b - a, J], BF16, name=f"x_grouped{a}", align_bytes=64) for a, b in X_CHUNKS]
+        x_codes = keep.tile([P, T], U32, name="x_codes", align_bytes=64)
+        x_scales = keep.tile([P, T], U8, name="x_scales", align_bytes=64)
+        w2_grouped = [keep.tile([P, N, J], BF16, name=f"w2_grouped{g}", align_bytes=64) for g in range(2)]
+        w2_codes = [keep.tile([P, N], U32, name=f"w2_codes{g}", align_bytes=64) for g in range(2)]
+        w2_scales = [keep.tile([P, N], U8, name=f"w2_scales{g}", align_bytes=64) for g in range(2)]
+
+        def group_w1(copy, g, c, ma, mb):
+            m0 = c * (WC // J)
+            copy(
+                out=w1_grouped[g][:, :, m0 + ma : m0 + mb, :].rearrange("p t m j -> p m j t"),
+                in_=w1_raw[g][c][:, :, J * ma : J * mb].rearrange("p j (m t) -> p m j t", t=J),
+            )
+
+        def quantize_w1(g):
+            nc.vector.quantize_mx(
+                out=w1_codes[g][:].rearrange("p t m -> p (t m)").bitcast(FP8X4),
+                scales=w1_scales[g][:].rearrange("p t m -> p (t m)"),
+                in_=w1_grouped[g][:].rearrange("p t m j -> p (t m j)"),
+            )
+
+        def group_cols(copy, dst, src, a, b):
+            copy(
+                out=dst[:, a:b, :].rearrange("p (c i) j -> p c j i", i=4),
+                in_=src[:, :, a:b].rearrange("p j (c i) -> p c j i", i=4),
+            )
+
+        def quantize_cols(codes, scales, grouped, c0, c1, g0):
+            nc.vector.quantize_mx(
+                out=codes[:, c0:c1].bitcast(FP8X4),
+                scales=scales[:, c0:c1],
+                in_=grouped[:, g0 : g0 + c1 - c0, :].rearrange("p n j -> p (n j)"),
+            )
+
+        vcopy, scopy = nc.vector.tensor_copy, nc.scalar.copy
+
+        h = [[keep.tile([P, T], F32, name=f"h{g}_{t}") for t in range(J)] for g in range(2)]
+
+        def project(g, t, n0, n1):
+            bank = psum.tile([P, 512], F32, name="bank")
+            nc.tensor.matmul_mx(
+                out=bank[:, : n1 - n0],
+                lhsT=w1_codes[g][:, t, :].bitcast(FP8X4),
+                lhsT_scale=w1_scales[g][:, t, :],
+                rhs=x_codes[:, n0:n1].bitcast(FP8X4),
+                rhs_scale=x_scales[:, n0:n1],
+                start=True,
+                stop=True,
+            )
+            nc.scalar.copy(out=h[g][t][:, n0:n1], in_=bank[:, : n1 - n0])
+
+        W_V = 44
+        for c in range(2):
+            group_w1(vcopy, 0, c, 0, W_V)
+            group_w1(scopy, 0, c, W_V, WC // J)
+        quantize_w1(0)
+        for c, (a, b) in enumerate(X_CHUNKS):
+            x_v = (b - a) * 11 // 16
+            group_cols(vcopy, x_grouped[c], x_raw[c], 0, x_v)
+            group_cols(scopy, x_grouped[c], x_raw[c], x_v, b - a)
+            quantize_cols(x_codes, x_scales, x_grouped[c], a, b, 0)
+            project(0, 0, a, b)
+        for t in range(1, J):
+            project(0, t, 0, T)
+
+        prods = [[keep.tile([P, J, V], F32, name=f"prod{g}_{d}") for d in range(D)] for g in range(2)]
+        sums = [[keep.tile([P, J, V], F32, name=f"sum{g}_{s}") for s in range(2)] for g in range(2)]
+        z_grouped = [keep.tile([P, V, J], BF16, name=f"z_grouped{g}", align_bytes=64) for g in range(2)]
+        z_codes = [keep.tile([P, V], U32, name=f"z_codes{g}", align_bytes=64) for g in range(2)]
+        z_scales = [keep.tile([P, V], U8, name=f"z_scales{g}", align_bytes=64) for g in range(2)]
+
+        def gather(g, d, t, v0=0, v1=V):
+            offs = pos[d][:] if v1 - v0 == V else pos[d][:, v0 // 16 : v1 // 16]
+            nc.vector.tensor_tensor(prods[g][d][:, t, v0:v1], h[g][t][:].indirect(offs), gates[d][:, v0:v1], MULT)
+
+        def add(dst, a, b):
+            nc.vector.tensor_tensor(
+                dst[:].rearrange("p t v -> p (t v)"), a[:].rearrange("p t v -> p (t v)"), b[:].rearrange("p t v -> p (t v)"), ADD
+            )
+
+        def last_add(g, v0, v1):
+            nc.vector.tensor_tensor(
+                z_grouped[g][:, v0:v1, :].rearrange("p (c i) t -> p c t i", i=4),
+                sums[g][1][:, :, v0:v1].rearrange("p t (c i) -> p c t i", i=4),
+                prods[g][3][:, :, v0:v1].rearrange("p t (c i) -> p c t i", i=4),
+                ADD,
+            )
+
+        acc = {}
+
+        def second(g, half):
+            for a in range(N // P):
+                if g == 0:
+                    acc[a, half] = psum.tile([P, 512], F32, name="bank")
+                nc.tensor.matmul_mx(
+                    out=acc[a, half][:, :VH],
+                    lhsT=w2_codes[g][:, a * P : (a + 1) * P].bitcast(FP8X4),
+                    lhsT_scale=w2_scales[g][:, a * P : (a + 1) * P],
+                    rhs=z_codes[g][:, half * VH : (half + 1) * VH].bitcast(FP8X4),
+                    rhs_scale=z_scales[g][:, half * VH : (half + 1) * VH],
+                    start=(g == 0),
+                    stop=(g == 1),
+                )
+
+        def emit(half, pair, copy, dma):
+            o = keep.tile([P, 2, VH], F32, name=f"o{half}_{pair}")
+            for b in range(2):
+                copy(out=o[:, b, :], in_=acc[2 * pair + b, half][:, :VH])
+            dma(out=out_view[:, 2 * pair : 2 * pair + 2, half * VH : (half + 1) * VH], in_=o[:])
+
+        for t in range(J):
+            for d in range(2):
+                gather(0, d, t)
+        for c in range(2):
+            group_w1(scopy, 1, c, 0, WC // J)
+        gather(0, 2, 0)
+        add(sums[0][0], prods[0][0], prods[0][1])
+        gather(0, 2, 1)
+        quantize_w1(1)
+        for t in range(J):
+            project(1, t, 0, T)
+        gather(0, 2, 2)
+        gather(0, 2, 3)
+        gather(0, 3, 0)
+        add(sums[0][1], sums[0][0], prods[0][2])
+        gather(0, 3, 1)
+        group_cols(scopy, w2_grouped[0], w2_raw[0], 0, N)
+        quantize_cols(w2_codes[0], w2_scales[0], w2_grouped[0], 0, N, 0)
+        gather(0, 3, 2)
+        gather(0, 3, 3)
+
+        gather(1, 0, 0)
+        last_add(0, 0, V)
+        gather(1, 0, 1)
+        quantize_cols(z_codes[0], z_scales[0], z_grouped[0], 0, V, 0)
+        for half in range(2):
+            second(0, half)
+        gather(1, 0, 2)
+        gather(1, 0, 3)
+        group_cols(scopy, w2_grouped[1], w2_raw[1], 0, N)
+        gather(1, 1, 0)
+        gather(1, 1, 1)
+        quantize_cols(w2_codes[1], w2_scales[1], w2_grouped[1], 0, N, 0)
+        gather(1, 1, 2)
+        gather(1, 1, 3)
+        gather(1, 2, 0)
+        add(sums[1][0], prods[1][0], prods[1][1])
+        for t in range(1, J):
+            gather(1, 2, t)
+        gather(1, 3, 0, 0, VH)
+        add(sums[1][1], sums[1][0], prods[1][2])
+        for t in range(1, J):
+            gather(1, 3, t, 0, VH)
+        gather(1, 3, 0, VH, V)
+        last_add(1, 0, VH)
+        for t in range(1, J):
+            gather(1, 3, t, VH, V)
+        quantize_cols(z_codes[1], z_scales[1], z_grouped[1], 0, VH, 0)
+        second(1, 0)
+        for pair in range(2):
+            emit(0, pair, nc.scalar.copy, nc.sync.dma_start)
+        Q = VH // 2
+        last_add(1, VH, VH + Q)
+        last_add(1, VH + Q, V)
+        quantize_cols(z_codes[1], z_scales[1], z_grouped[1], VH, VH + Q, VH)
+        quantize_cols(z_codes[1], z_scales[1], z_grouped[1], VH + Q, V, VH + Q)
+        second(1, 1)
+        emit(1, 0, nc.vector.tensor_copy, nc.sync.dma_start)
+        emit(1, 1, nc.scalar.copy, nc.scalar.dma_start)

@@ -17,8 +17,7 @@ FLOPS = 2 * K * H * T + 2 * H * N * V
 P = 128
 J = 4
 KP = P * J
-X_CHUNKS = ((0, 256), (256, 384), (384, 512))
-WC = 256
+X_V = 352
 VH = 128
 
 
@@ -32,8 +31,9 @@ def tile_picked_gcn_mlp_none_sub_l_kernel(tc, xT, w1, w2, gate, pos1, pos2, pos3
         pos = [lists.tile([P, V // 16], U16, name=f"pos{d}") for d in range(D)]
         gates = [keep.tile([P, V], F32, name=f"gate{d}") for d in range(D)]
 
-        x_raw = [keep.tile([P, J, b - a], F32, name=f"x_raw{a}") for a, b in X_CHUNKS]
-        w1_raw = [[keep.tile([P, J, WC], F32, name=f"w1_raw{g}_{c}") for c in range(2)] for g in range(2)]
+        x_raw = keep.tile([P, J, T], F32, name="x_raw")
+        w1_first = [keep.tile([P, J // 2, KP], F32, name=f"w1_first{c}") for c in range(2)]
+        w1_rest = keep.tile([P, J, KP], F32, name="w1_rest")
         w2_raw = [keep.tile([P, J, N], F32, name=f"w2_raw{g}") for g in range(2)]
 
         x_view = xT.rearrange("(p j) t -> p j t", j=J)
@@ -41,51 +41,43 @@ def tile_picked_gcn_mlp_none_sub_l_kernel(tc, xT, w1, w2, gate, pos1, pos2, pos3
         w2_view = w2.rearrange("(g p j) n -> g p j n", g=2, j=J)
         out_view = out.rearrange("(a p) v -> p a v", p=P)
 
-        def load_w1(g, c):
-            i0 = g * KP + c * WC
-            nc.sync.dma_start(w1_raw[g][c][:], w1_view[:, :, i0 : i0 + WC])
-
-        def load_x(c):
-            a, b = X_CHUNKS[c]
-            nc.sync.dma_start(x_raw[c][:], x_view[:, :, a:b])
-
-        load_w1(0, 0)
-        load_w1(0, 1)
-        load_x(0)
-        nc.sync.dma_start(pos[0][:], pos1)
-        load_x(1)
-        load_x(2)
-        nc.sync.dma_start(gates[0][:], gate[0])
-        for d, src in ((1, pos2), (2, pos3), (3, pos4)):
+        nc.sync.dma_start(x_raw[:], x_view)
+        for c in range(2):
+            nc.sync.dma_start(w1_first[c][:], w1_view[:, 2 * c : 2 * c + 2, 0:KP])
+        for d, src in enumerate((pos1, pos2, pos3, pos4)):
             nc.sync.dma_start(pos[d][:], src)
             nc.sync.dma_start(gates[d][:], gate[d])
-        load_w1(1, 0)
-        load_w1(1, 1)
+        nc.sync.dma_start(w1_rest[:], w1_view[:, :, KP:H])
         for g in range(2):
             nc.sync.dma_start(w2_raw[g][:], w2_view[g])
 
         w1_grouped = [keep.tile([P, J, P, J], BF16, name=f"w1_grouped{g}", align_bytes=64) for g in range(2)]
         w1_codes = [keep.tile([P, J, P], U32, name=f"w1_codes{g}", align_bytes=64) for g in range(2)]
         w1_scales = [keep.tile([P, J, P], U8, name=f"w1_scales{g}", align_bytes=64) for g in range(2)]
-        x_grouped = [keep.tile([P, b - a, J], BF16, name=f"x_grouped{a}", align_bytes=64) for a, b in X_CHUNKS]
+        x_grouped = keep.tile([P, T, J], BF16, name="x_grouped", align_bytes=64)
         x_codes = keep.tile([P, T], U32, name="x_codes", align_bytes=64)
         x_scales = keep.tile([P, T], U8, name="x_scales", align_bytes=64)
         w2_grouped = [keep.tile([P, N, J], BF16, name=f"w2_grouped{g}", align_bytes=64) for g in range(2)]
         w2_codes = [keep.tile([P, N], U32, name=f"w2_codes{g}", align_bytes=64) for g in range(2)]
         w2_scales = [keep.tile([P, N], U8, name=f"w2_scales{g}", align_bytes=64) for g in range(2)]
 
-        def group_w1(copy, g, c, ma, mb):
-            m0 = c * (WC // J)
+        def group_w1_first(copy, c, t):
             copy(
-                out=w1_grouped[g][:, :, m0 + ma : m0 + mb, :].rearrange("p t m j -> p m j t"),
-                in_=w1_raw[g][c][:, :, J * ma : J * mb].rearrange("p j (m t) -> p m j t", t=J),
+                out=w1_grouped[0][:, t, :, 2 * c : 2 * c + 2],
+                in_=w1_first[c][:].rearrange("p j (m t) -> p t m j", t=J)[:, t, :, :],
             )
 
-        def quantize_w1(g):
+        def group_w1_rest(copy, ma, mb):
+            copy(
+                out=w1_grouped[1][:, :, ma:mb, :].rearrange("p t m j -> p m j t"),
+                in_=w1_rest[:, :, J * ma : J * mb].rearrange("p j (m t) -> p m j t", t=J),
+            )
+
+        def quantize_w1(g, t0, t1):
             nc.vector.quantize_mx(
-                out=w1_codes[g][:].rearrange("p t m -> p (t m)").bitcast(FP8X4),
-                scales=w1_scales[g][:].rearrange("p t m -> p (t m)"),
-                in_=w1_grouped[g][:].rearrange("p t m j -> p (t m j)"),
+                out=w1_codes[g][:, t0:t1, :].rearrange("p t m -> p (t m)").bitcast(FP8X4),
+                scales=w1_scales[g][:, t0:t1, :].rearrange("p t m -> p (t m)"),
+                in_=w1_grouped[g][:, t0:t1, :, :].rearrange("p t m j -> p (t m j)"),
             )
 
         def group_cols(copy, dst, src, a, b):
@@ -105,7 +97,7 @@ def tile_picked_gcn_mlp_none_sub_l_kernel(tc, xT, w1, w2, gate, pos1, pos2, pos3
 
         h = [[keep.tile([P, T], F32, name=f"h{g}_{t}") for t in range(J)] for g in range(2)]
 
-        def project(g, t, n0, n1):
+        def project(g, t, n0, n1, copy=nc.scalar.copy):
             bank = psum.tile([P, 512], F32, name="bank")
             nc.tensor.matmul_mx(
                 out=bank[:, : n1 - n0],
@@ -116,21 +108,23 @@ def tile_picked_gcn_mlp_none_sub_l_kernel(tc, xT, w1, w2, gate, pos1, pos2, pos3
                 start=True,
                 stop=True,
             )
-            nc.scalar.copy(out=h[g][t][:, n0:n1], in_=bank[:, : n1 - n0])
+            copy(out=h[g][t][:, n0:n1], in_=bank[:, : n1 - n0])
 
-        W_V = 44
-        for c in range(2):
-            group_w1(vcopy, 0, c, 0, W_V)
-            group_w1(scopy, 0, c, W_V, WC // J)
-        quantize_w1(0)
-        for c, (a, b) in enumerate(X_CHUNKS):
-            x_v = (b - a) * 11 // 16
-            group_cols(vcopy, x_grouped[c], x_raw[c], 0, x_v)
-            group_cols(scopy, x_grouped[c], x_raw[c], x_v, b - a)
-            quantize_cols(x_codes, x_scales, x_grouped[c], a, b, 0)
-            project(0, 0, a, b)
-        for t in range(1, J):
-            project(0, t, 0, T)
+        group_cols(vcopy, x_grouped, x_raw, 0, X_V)
+        group_cols(scopy, x_grouped, x_raw, X_V, T)
+        for n in range(2):
+            quantize_cols(x_codes, x_scales, x_grouped, n * 256, (n + 1) * 256, n * 256)
+        for t in range(J):
+            group_w1_first(vcopy if t < 2 else scopy, 0, t)
+        group_w1_first(vcopy, 1, 0)
+        quantize_w1(0, 0, 1)
+        group_w1_first(scopy, 1, 1)
+        project(0, 0, 0, 256)
+        project(0, 0, 256, 512, vcopy)
+        quantize_w1(0, 1, 2)
+        group_w1_first(scopy, 1, 2)
+        project(0, 1, 0, T)
+        group_w1_first(scopy, 1, 3)
 
         prods = [[keep.tile([P, J, V], F32, name=f"prod{g}_{d}") for d in range(D)] for g in range(2)]
         sums = [[keep.tile([P, J, V], F32, name=f"sum{g}_{s}") for s in range(2)] for g in range(2)]
@@ -177,15 +171,20 @@ def tile_picked_gcn_mlp_none_sub_l_kernel(tc, xT, w1, w2, gate, pos1, pos2, pos3
                 copy(out=o[:, b, :], in_=acc[2 * pair + b, half][:, :VH])
             dma(out=out_view[:, 2 * pair : 2 * pair + 2, half * VH : (half + 1) * VH], in_=o[:])
 
-        for t in range(J):
+        gather(0, 0, 0)
+        gather(0, 1, 0)
+        quantize_w1(0, 2, 4)
+        for t in (2, 3):
+            project(0, t, 0, T)
+        for t in range(1, J):
             for d in range(2):
                 gather(0, d, t)
-        for c in range(2):
-            group_w1(scopy, 1, c, 0, WC // J)
+        for m in range(0, P, 64):
+            group_w1_rest(scopy, m, m + 64)
         gather(0, 2, 0)
         add(sums[0][0], prods[0][0], prods[0][1])
         gather(0, 2, 1)
-        quantize_w1(1)
+        quantize_w1(1, 0, J)
         for t in range(J):
             project(1, t, 0, T)
         gather(0, 2, 2)

@@ -183,55 +183,51 @@ def tile_picked_gcn_mlp_none_sub_l_kernel(tc, xT, w1, w2, gate, pos1, pos2, pos3
             group_w1_rest(scopy, m, m + 64)
         gather(0, 2, 0)
         add(sums[0][0], prods[0][0], prods[0][1])
-        gather(0, 2, 1)
-        quantize_w1(1, 0, J)
-        for t in range(J):
-            project(1, t, 0, T)
-        gather(0, 2, 2)
-        gather(0, 2, 3)
+        for t in range(1, J):
+            gather(0, 2, t)
         gather(0, 3, 0)
         add(sums[0][1], sums[0][0], prods[0][2])
         gather(0, 3, 1)
-        group_cols(scopy, w2_grouped[0], w2_raw[0], 0, N)
-        quantize_cols(w2_codes[0], w2_scales[0], w2_grouped[0], 0, N, 0)
+        quantize_w1(1, 0, J)
+        for t in range(J):
+            project(1, t, 0, T)
         gather(0, 3, 2)
         gather(0, 3, 3)
+        for g in range(2):
+            group_cols(scopy, w2_grouped[g], w2_raw[g], 0, N)
 
         gather(1, 0, 0)
         last_add(0, 0, V)
-        gather(1, 0, 1)
-        quantize_cols(z_codes[0], z_scales[0], z_grouped[0], 0, V, 0)
-        for half in range(2):
-            second(0, half)
-        gather(1, 0, 2)
-        gather(1, 0, 3)
-        group_cols(scopy, w2_grouped[1], w2_raw[1], 0, N)
+        for t in range(1, J):
+            gather(1, 0, t)
         gather(1, 1, 0)
-        gather(1, 1, 1)
-        quantize_cols(w2_codes[1], w2_scales[1], w2_grouped[1], 0, N, 0)
-        gather(1, 1, 2)
-        gather(1, 1, 3)
+        quantize_cols(z_codes[0], z_scales[0], z_grouped[0], 0, V, 0)
+        for t in range(1, J):
+            gather(1, 1, t)
         gather(1, 2, 0)
         add(sums[1][0], prods[1][0], prods[1][1])
-        for t in range(1, J):
-            gather(1, 2, t)
+        gather(1, 2, 1)
+        quantize_cols(w2_codes[0], w2_scales[0], w2_grouped[0], 0, N, 0)
+        for half in range(2):
+            second(0, half)
+        gather(1, 2, 2)
+        gather(1, 2, 3)
         gather(1, 3, 0, 0, VH)
         add(sums[1][1], sums[1][0], prods[1][2])
         for t in range(1, J):
             gather(1, 3, t, 0, VH)
+        quantize_cols(w2_codes[1], w2_scales[1], w2_grouped[1], 0, N, 0)
         gather(1, 3, 0, VH, V)
         last_add(1, 0, VH)
-        for t in range(1, J):
-            gather(1, 3, t, VH, V)
+        gather(1, 3, 1, VH, V)
         quantize_cols(z_codes[1], z_scales[1], z_grouped[1], 0, VH, 0)
         second(1, 0)
         for pair in range(2):
             emit(0, pair, nc.scalar.copy, nc.sync.dma_start)
-        Q = VH // 2
-        last_add(1, VH, VH + Q)
-        last_add(1, VH + Q, V)
-        quantize_cols(z_codes[1], z_scales[1], z_grouped[1], VH, VH + Q, VH)
-        quantize_cols(z_codes[1], z_scales[1], z_grouped[1], VH + Q, V, VH + Q)
+        gather(1, 3, 2, VH, V)
+        gather(1, 3, 3, VH, V)
+        last_add(1, VH, V)
+        quantize_cols(z_codes[1], z_scales[1], z_grouped[1], VH, V, VH)
         second(1, 1)
         emit(1, 0, nc.vector.tensor_copy, nc.sync.dma_start)
         emit(1, 1, nc.scalar.copy, nc.scalar.dma_start)

@@ -151,25 +151,24 @@ def tile_picked_gcn_mlp_none_sub_l_kernel(tc, xT, w1, w2, gate, pos1, pos2, pos3
 
         acc = {}
 
-        def second(g, half):
+        def second(g):
             for a in range(N // P):
                 if g == 0:
-                    acc[a, half] = psum.tile([P, 512], F32, name="bank")
+                    acc[a] = psum.tile([P, 512], F32, name="bank")
                 nc.tensor.matmul_mx(
-                    out=acc[a, half][:, :VH],
+                    out=acc[a][:, :V],
                     lhsT=w2_codes[g][:, a * P : (a + 1) * P].bitcast(FP8X4),
                     lhsT_scale=w2_scales[g][:, a * P : (a + 1) * P],
-                    rhs=z_codes[g][:, half * VH : (half + 1) * VH].bitcast(FP8X4),
-                    rhs_scale=z_scales[g][:, half * VH : (half + 1) * VH],
+                    rhs=z_codes[g][:].bitcast(FP8X4),
+                    rhs_scale=z_scales[g][:],
                     start=(g == 0),
                     stop=(g == 1),
                 )
 
-        def emit(half, pair, copy, dma):
-            o = keep.tile([P, 2, VH], F32, name=f"o{half}_{pair}")
-            for b in range(2):
-                copy(out=o[:, b, :], in_=acc[2 * pair + b, half][:, :VH])
-            dma(out=out_view[:, 2 * pair : 2 * pair + 2, half * VH : (half + 1) * VH], in_=o[:])
+        def emit(a, copy, dma):
+            o = keep.tile([P, V], F32, name=f"o{a}")
+            copy(out=o[:], in_=acc[a][:, :V])
+            dma(out=out_view[:, a, :], in_=o[:])
 
         gather(0, 0, 0)
         gather(0, 1, 0)
@@ -208,26 +207,21 @@ def tile_picked_gcn_mlp_none_sub_l_kernel(tc, xT, w1, w2, gate, pos1, pos2, pos3
         add(sums[1][0], prods[1][0], prods[1][1])
         gather(1, 2, 1)
         quantize_cols(w2_codes[0], w2_scales[0], w2_grouped[0], 0, N, 0)
-        for half in range(2):
-            second(0, half)
+        second(0)
         gather(1, 2, 2)
         gather(1, 2, 3)
-        gather(1, 3, 0, 0, VH)
+        gather(1, 3, 0)
         add(sums[1][1], sums[1][0], prods[1][2])
-        for t in range(1, J):
-            gather(1, 3, t, 0, VH)
+        gather(1, 3, 1)
         quantize_cols(w2_codes[1], w2_scales[1], w2_grouped[1], 0, N, 0)
-        gather(1, 3, 0, VH, V)
+        gather(1, 3, 2)
+        gather(1, 3, 3)
         last_add(1, 0, VH)
-        gather(1, 3, 1, VH, V)
-        quantize_cols(z_codes[1], z_scales[1], z_grouped[1], 0, VH, 0)
-        second(1, 0)
-        for pair in range(2):
-            emit(0, pair, nc.scalar.copy, nc.sync.dma_start)
-        gather(1, 3, 2, VH, V)
-        gather(1, 3, 3, VH, V)
         last_add(1, VH, V)
+        quantize_cols(z_codes[1], z_scales[1], z_grouped[1], 0, VH, 0)
         quantize_cols(z_codes[1], z_scales[1], z_grouped[1], VH, V, VH)
-        second(1, 1)
-        emit(1, 0, nc.vector.tensor_copy, nc.sync.dma_start)
-        emit(1, 1, nc.scalar.copy, nc.scalar.dma_start)
+        second(1)
+        emit(0, nc.vector.tensor_copy, nc.sync.dma_start)
+        emit(1, nc.scalar.copy, nc.scalar.dma_start)
+        emit(2, nc.vector.tensor_copy, nc.sync.dma_start)
+        emit(3, nc.scalar.copy, nc.scalar.dma_start)

from contextlib import ExitStack

import concourse.mybir as mybir

F32 = mybir.dt.float32
BF16 = mybir.dt.bfloat16
U32 = mybir.dt.uint32
U16 = mybir.dt.uint16
U8 = mybir.dt.uint8
FP8X4 = mybir.dt.float8_e4m3fn_x4
MULT = mybir.AluOpType.mult
ADD = mybir.AluOpType.add

K, T, D, V, H, N = 512, 512, 4, 256, 1024, 512
FLOPS = 2 * K * H * T + 2 * H * N * V

P = 128
J = 4
KP = P * J
X_V = 352
VH = 128


def tile_picked_gcn_mlp_none_sub_l_kernel(tc, xT, w1, w2, gate, pos1, pos2, pos3, pos4, out):
    nc = tc.nc
    with ExitStack() as ctx:
        lists = ctx.enter_context(tc.tile_pool(name="lists", bufs=1))
        keep = ctx.enter_context(tc.tile_pool(name="keep", bufs=1))
        psum = ctx.enter_context(tc.psum_pool(name="psum", bufs=8))

        pos = [lists.tile([P, V // 16], U16, name=f"pos{d}") for d in range(D)]
        gates = [keep.tile([P, V], F32, name=f"gate{d}") for d in range(D)]

        x_raw = keep.tile([P, J, T], F32, name="x_raw")
        w1_first = [keep.tile([P, J // 2, KP], F32, name=f"w1_first{c}") for c in range(2)]
        w1_rest = keep.tile([P, J, KP], F32, name="w1_rest")
        w2_raw = [keep.tile([P, J, N], F32, name=f"w2_raw{g}") for g in range(2)]

        x_view = xT.rearrange("(p j) t -> p j t", j=J)
        w1_view = w1.rearrange("(p j) i -> p j i", j=J)
        w2_view = w2.rearrange("(g p j) n -> g p j n", g=2, j=J)
        out_view = out.rearrange("(a p) v -> p a v", p=P)

        nc.sync.dma_start(x_raw[:], x_view)
        for c in range(2):
            nc.sync.dma_start(w1_first[c][:], w1_view[:, 2 * c : 2 * c + 2, 0:KP])
        for d, src in enumerate((pos1, pos2, pos3, pos4)):
            nc.sync.dma_start(pos[d][:], src)
            nc.sync.dma_start(gates[d][:], gate[d])
        nc.sync.dma_start(w1_rest[:], w1_view[:, :, KP:H])
        for g in range(2):
            nc.sync.dma_start(w2_raw[g][:], w2_view[g])

        w1_grouped = [keep.tile([P, J, P, J], BF16, name=f"w1_grouped{g}", align_bytes=64) for g in range(2)]
        w1_codes = [keep.tile([P, J, P], U32, name=f"w1_codes{g}", align_bytes=64) for g in range(2)]
        w1_scales = [keep.tile([P, J, P], U8, name=f"w1_scales{g}", align_bytes=64) for g in range(2)]
        x_grouped = keep.tile([P, T, J], BF16, name="x_grouped", align_bytes=64)
        x_codes = keep.tile([P, T], U32, name="x_codes", align_bytes=64)
        x_scales = keep.tile([P, T], U8, name="x_scales", align_bytes=64)
        w2_grouped = [keep.tile([P, N, J], BF16, name=f"w2_grouped{g}", align_bytes=64) for g in range(2)]
        w2_codes = [keep.tile([P, N], U32, name=f"w2_codes{g}", align_bytes=64) for g in range(2)]
        w2_scales = [keep.tile([P, N], U8, name=f"w2_scales{g}", align_bytes=64) for g in range(2)]

        def group_w1_first(copy, c, t):
            copy(
                out=w1_grouped[0][:, t, :, 2 * c : 2 * c + 2],
                in_=w1_first[c][:].rearrange("p j (m t) -> p t m j", t=J)[:, t, :, :],
            )

        def group_w1_rest(copy, ma, mb):
            copy(
                out=w1_grouped[1][:, :, ma:mb, :].rearrange("p t m j -> p m j t"),
                in_=w1_rest[:, :, J * ma : J * mb].rearrange("p j (m t) -> p m j t", t=J),
            )

        def quantize_w1(g, t0, t1):
            nc.vector.quantize_mx(
                out=w1_codes[g][:, t0:t1, :].rearrange("p t m -> p (t m)").bitcast(FP8X4),
                scales=w1_scales[g][:, t0:t1, :].rearrange("p t m -> p (t m)"),
                in_=w1_grouped[g][:, t0:t1, :, :].rearrange("p t m j -> p (t m j)"),
            )

        def group_cols(copy, dst, src, a, b):
            copy(
                out=dst[:, a:b, :].rearrange("p (c i) j -> p c j i", i=4),
                in_=src[:, :, a:b].rearrange("p j (c i) -> p c j i", i=4),
            )

        def quantize_cols(codes, scales, grouped, c0, c1, g0):
            nc.vector.quantize_mx(
                out=codes[:, c0:c1].bitcast(FP8X4),
                scales=scales[:, c0:c1],
                in_=grouped[:, g0 : g0 + c1 - c0, :].rearrange("p n j -> p (n j)"),
            )

        vcopy, scopy = nc.vector.tensor_copy, nc.scalar.copy

        h = [[keep.tile([P, T], F32, name=f"h{g}_{t}") for t in range(J)] for g in range(2)]

        def project(g, t, n0, n1, copy=nc.scalar.copy):
            bank = psum.tile([P, 512], F32, name="bank")
            nc.tensor.matmul_mx(
                out=bank[:, : n1 - n0],
                lhsT=w1_codes[g][:, t, :].bitcast(FP8X4),
                lhsT_scale=w1_scales[g][:, t, :],
                rhs=x_codes[:, n0:n1].bitcast(FP8X4),
                rhs_scale=x_scales[:, n0:n1],
                start=True,
                stop=True,
            )
            copy(out=h[g][t][:, n0:n1], in_=bank[:, : n1 - n0])

        group_cols(vcopy, x_grouped, x_raw, 0, X_V)
        group_cols(scopy, x_grouped, x_raw, X_V, T)
        for n in range(2):
            quantize_cols(x_codes, x_scales, x_grouped, n * 256, (n + 1) * 256, n * 256)
        for t in range(J):
            group_w1_first(vcopy if t < 2 else scopy, 0, t)
        group_w1_first(vcopy, 1, 0)
        quantize_w1(0, 0, 1)
        group_w1_first(scopy, 1, 1)
        project(0, 0, 0, 256)
        project(0, 0, 256, 512, vcopy)
        quantize_w1(0, 1, 2)
        group_w1_first(scopy, 1, 2)
        project(0, 1, 0, T)
        group_w1_first(scopy, 1, 3)

        prods = [[keep.tile([P, J, V], F32, name=f"prod{g}_{d}") for d in range(D)] for g in range(2)]
        sums = [[keep.tile([P, J, V], F32, name=f"sum{g}_{s}") for s in range(2)] for g in range(2)]
        z_grouped = [keep.tile([P, V, J], BF16, name=f"z_grouped{g}", align_bytes=64) for g in range(2)]
        z_codes = [keep.tile([P, V], U32, name=f"z_codes{g}", align_bytes=64) for g in range(2)]
        z_scales = [keep.tile([P, V], U8, name=f"z_scales{g}", align_bytes=64) for g in range(2)]

        def gather(g, d, t, v0=0, v1=V):
            offs = pos[d][:] if v1 - v0 == V else pos[d][:, v0 // 16 : v1 // 16]
            nc.vector.tensor_tensor(prods[g][d][:, t, v0:v1], h[g][t][:].indirect(offs), gates[d][:, v0:v1], MULT)

        def add(dst, a, b):
            nc.vector.tensor_tensor(
                dst[:].rearrange("p t v -> p (t v)"), a[:].rearrange("p t v -> p (t v)"), b[:].rearrange("p t v -> p (t v)"), ADD
            )

        def last_add(g, v0, v1):
            nc.vector.tensor_tensor(
                z_grouped[g][:, v0:v1, :].rearrange("p (c i) t -> p c t i", i=4),
                sums[g][1][:, :, v0:v1].rearrange("p t (c i) -> p c t i", i=4),
                prods[g][3][:, :, v0:v1].rearrange("p t (c i) -> p c t i", i=4),
                ADD,
            )

        acc = {}

        def second(g):
            for a in range(N // P):
                if g == 0:
                    acc[a] = psum.tile([P, 512], F32, name="bank")
                nc.tensor.matmul_mx(
                    out=acc[a][:, :V],
                    lhsT=w2_codes[g][:, a * P : (a + 1) * P].bitcast(FP8X4),
                    lhsT_scale=w2_scales[g][:, a * P : (a + 1) * P],
                    rhs=z_codes[g][:].bitcast(FP8X4),
                    rhs_scale=z_scales[g][:],
                    start=(g == 0),
                    stop=(g == 1),
                )

        def emit(a, copy, dma):
            o = keep.tile([P, V], F32, name=f"o{a}")
            copy(out=o[:], in_=acc[a][:, :V])
            dma(out=out_view[:, a, :], in_=o[:])

        gather(0, 0, 0)
        gather(0, 1, 0)
        quantize_w1(0, 2, 4)
        for t in (2, 3):
            project(0, t, 0, T)
        for t in range(1, J):
            for d in range(2):
                gather(0, d, t)
        for m in range(0, P, 64):
            group_w1_rest(scopy, m, m + 64)
        gather(0, 2, 0)
        add(sums[0][0], prods[0][0], prods[0][1])
        for t in range(1, J):
            gather(0, 2, t)
        gather(0, 3, 0)
        add(sums[0][1], sums[0][0], prods[0][2])
        gather(0, 3, 1)
        quantize_w1(1, 0, J)
        for t in range(J):
            project(1, t, 0, T)
        gather(0, 3, 2)
        gather(0, 3, 3)
        for g in range(2):
            group_cols(scopy, w2_grouped[g], w2_raw[g], 0, N)

        gather(1, 0, 0)
        last_add(0, 0, V)
        for t in range(1, J):
            gather(1, 0, t)
        gather(1, 1, 0)
        quantize_cols(z_codes[0], z_scales[0], z_grouped[0], 0, V, 0)
        for t in range(1, J):
            gather(1, 1, t)
        gather(1, 2, 0)
        add(sums[1][0], prods[1][0], prods[1][1])
        gather(1, 2, 1)
        quantize_cols(w2_codes[0], w2_scales[0], w2_grouped[0], 0, N, 0)
        second(0)
        gather(1, 2, 2)
        gather(1, 2, 3)
        gather(1, 3, 0)
        add(sums[1][1], sums[1][0], prods[1][2])
        gather(1, 3, 1)
        quantize_cols(w2_codes[1], w2_scales[1], w2_grouped[1], 0, N, 0)
        gather(1, 3, 2)
        gather(1, 3, 3)
        last_add(1, 0, VH)
        last_add(1, VH, V)
        quantize_cols(z_codes[1], z_scales[1], z_grouped[1], 0, VH, 0)
        quantize_cols(z_codes[1], z_scales[1], z_grouped[1], VH, V, VH)
        second(1)
        emit(0, nc.vector.tensor_copy, nc.sync.dma_start)
        emit(1, nc.scalar.copy, nc.scalar.dma_start)
        emit(2, nc.vector.tensor_copy, nc.sync.dma_start)
        emit(3, nc.scalar.copy, nc.scalar.dma_start)
